import numpy as np
import ml_dtypes


def mxq(x, axis, fmt="e4m3"):
    dtype, down = {"e4m3": (ml_dtypes.float8_e4m3fn, 7), "e5m2": (ml_dtypes.float8_e5m2, 14)}[fmt]
    v = np.moveaxis(np.asarray(x, np.float32).astype(ml_dtypes.bfloat16).astype(np.float64), axis, -1)
    blocks = v.reshape(v.shape[:-1] + (-1, 32))
    amax = np.abs(blocks).max(-1, keepdims=True)
    byte = np.maximum(np.where(amax > 0, np.frexp(amax)[1] - 1 + 127, 0) - down, 1)
    scale = np.exp2(byte - 127.0)
    codes = (blocks / scale).astype(np.float32).astype(dtype).astype(np.float64)
    return np.moveaxis((codes * scale).reshape(v.shape), -1, axis)


WIDE = False


def mx_kscale(k):
    if not WIDE:
        return np.ones(k)
    levels = np.array([10, -10, 5, -5, 0])
    if k % 512:
        return np.exp2(np.random.permutation(np.resize(levels, k // 32))).repeat(32)
    a = np.empty((k // 512, 16))
    for p in range(k // 512):
        a[p, :8] = np.random.permutation(np.resize(levels, 8))
        for g in range(8):
            far = levels[np.abs(levels - a[p, g]) >= 10]
            a[p, g + 8] = far[np.random.randint(len(far))]
    return np.exp2(a.ravel()).repeat(32)


def f64(x):
    return np.asarray(x).astype(np.float64)


def striped8(idx):
    return np.asarray(idx).reshape(8, -1, 16).transpose(0, 2, 1).reshape(128, -1).astype(np.uint16)


def unstriped8(offs):
    return offs.reshape(8, 16, -1).transpose(0, 2, 1).reshape(8, -1).astype(np.int64)


def pick8(x, idx, run):
    r = np.arange(len(x))
    return x[r[:, None], idx[r % (8 * run) // run]]


E2M1 = np.array([0.0, 0.5, 1.0, 1.5, 2.0, 3.0, 4.0, 6.0, -0.0, -0.5, -1.0, -1.5, -2.0, -3.0, -4.0, -6.0])


def pack_weight(w, fmt):
    k, n = w.shape
    w = f64(np.asarray(w, np.float32).astype(ml_dtypes.bfloat16)).reshape(k // 32, 32, n)
    amax = np.abs(w).max(1)
    if fmt == "e4m3":
        byte = np.frexp(amax)[1] - 1 + 127 - 7
    else:
        mant, ex = np.frexp(amax / 6.0)
        byte = np.where(mant > 0.5, ex, ex - 1) + 127
    byte = np.clip(np.where(amax > 0, byte, 1), 1, 254)
    scaled = (w * np.exp2(127.0 - byte)[:, None, :]).reshape(k, n).astype(np.float32)
    by_word = np.ascontiguousarray(scaled.reshape(k // 512, 128, 4, n).transpose(0, 1, 3, 2))
    if fmt == "e4m3":
        words = by_word.astype(ml_dtypes.float8_e4m3fn).view(np.uint8)
    else:
        c = by_word.astype(ml_dtypes.float4_e2m1fn).view(np.uint8) & 0xF
        words = (c[..., 0::2] | (c[..., 1::2] << 4)).reshape(k // 512, 128, 2 * n)
    return np.ascontiguousarray(words), np.ascontiguousarray(byte.astype(np.uint8).reshape(k // 512, 16, n))


def unpack_weight(words, scales, fmt):
    g, _, n = scales.shape
    words = np.ascontiguousarray(words).reshape(g, 128, n, -1)
    if fmt == "e4m3":
        vals = words.view(ml_dtypes.float8_e4m3fn).astype(np.float64)
    else:
        nib = np.empty((g, 128, n, 4), np.uint8)
        nib[..., 0::2] = words & 0xF
        nib[..., 1::2] = words >> 4
        vals = E2M1[nib]
    vals = vals * np.repeat(np.exp2(scales.astype(np.float64) - 127.0), 8, axis=1)[..., None]
    return vals.transpose(0, 1, 3, 2).reshape(g * 512, n)


def bf(x):
    return np.asarray(x, np.float32).astype(ml_dtypes.bfloat16)


def planes(Y):
    r, m = Y.shape
    b = f64(bf(Y)).reshape(r // 32, 32, m)
    amax = np.abs(b).max(1)
    byte = np.clip(np.where(amax > 0, np.frexp(amax)[1] - 1 + 127 - 7, 1), 1, 254)
    codes = (b * np.exp2(127.0 - byte)[:, None, :]).reshape(r, m).astype(np.float32).astype(ml_dtypes.float8_e4m3fn).view(np.uint8)
    words = codes.reshape(r // 512, 128, 4, m).transpose(0, 1, 3, 2)
    return np.ascontiguousarray(words), np.ascontiguousarray(byte.astype(np.uint8).reshape(r // 512, 16, m))


K, T, J, N, B = 512, 512, 1024, 512, 128


def setup_inputs():
    n = np.random.standard_normal
    idx = np.stack([np.random.randint(0, T, J) for _ in range(8)])
    fk = mx_kscale(K)
    wp = pack_weight(n((K, N)) * 1 / np.sqrt(K) * fk[:, None], "e2m1")
    return {
        "xt": (n((K, T)) / fk[:, None]).astype(np.float32),
        "w_words": wp[0],
        "w_scales": wp[1],
        "lam": (np.random.uniform(0.2, 0.9, (N, 1))).astype(np.float32),
        "offs": striped8(idx),
    }


def reference(xt, w_words, w_scales, lam, offs):
    idx = unstriped8(offs)
    wu = unpack_weight(w_words, w_scales, "e2m1")
    xtq = mxq(f64(xt), 0, "e4m3")
    z = wu.T @ xtq
    u = pick8(z, idx, 64)
    y = u.reshape(N, B, J // B).max(axis=2) - f64(lam) * u.reshape(N, B, J // B).mean(axis=2)
    words, scales = planes(y)
    return y, words, scales

@@ -1,0 +1,141 @@
+from contextlib import ExitStack
+
+import concourse.mybir as mybir
+from concourse.masks import make_identity
+
+K, T, J, N, B = 512, 512, 1024, 512, 128
+FLOPS = 2 * K * N * T
+
+F32 = mybir.dt.float32
+BF16 = mybir.dt.bfloat16
+I32 = mybir.dt.int32
+U32 = mybir.dt.uint32
+U16 = mybir.dt.uint16
+U8 = mybir.dt.uint8
+FP8X4 = mybir.dt.float8_e4m3fn_x4
+FP4X4 = mybir.dt.float4_e2m1fn_x4
+ALU = mybir.AluOpType
+ACT = mybir.ActivationFunctionType
+
+P = 128
+PACK = 4
+GROUP = J // B
+HALVES = 2
+HALF_J = J // HALVES
+HALF_B = B // HALVES
+SPARE = 8
+TOKEN_PIECE = 256
+VECTOR_TOKENS = 160
+
+
+def tile_list_head_peaks_of_groups_pl_kernel(tc, xt, w_words, w_scales, lam, offs, out_0, out_1, out_2):
+    nc = tc.nc
+    with ExitStack() as ctx:
+        lists = ctx.enter_context(tc.tile_pool(name="lists", bufs=1))
+        keep = ctx.enter_context(tc.tile_pool(name="keep", bufs=1))
+        psum = ctx.enter_context(tc.psum_pool(name="psum", bufs=1))
+
+        pieces = T // TOKEN_PIECE
+        x_rows = xt.rearrange("(p j) t -> p j t", j=PACK)
+        x_raw = []
+        for s in range(pieces):
+            raw = keep.tile([P, PACK, TOKEN_PIECE], F32, name=f"x_raw{s}")
+            nc.scalar.dma_start(out=raw[:], in_=x_rows[:, :, s * TOKEN_PIECE : (s + 1) * TOKEN_PIECE])
+            x_raw.append(raw)
+
+        w_scales_raw = keep.tile([P, N], U8, align_bytes=64)
+        nc.gpsimd.memset(w_scales_raw[:].bitcast(I32), 0)
+        w_words_raw = keep.tile([P, 2 * N], U8, align_bytes=64)
+        nc.sync.dma_start(out=w_words_raw[:].bitcast(I32), in_=w_words[0].bitcast(I32))
+        for q in range(4):
+            nc.sync.dma_start(
+                out=w_scales_raw[32 * q : 32 * q + 4, :].bitcast(I32),
+                in_=w_scales[0, 4 * q : 4 * q + 4, :].bitcast(I32),
+            )
+        offsets = lists.tile([P, J // 16], U16, name="offsets")
+        nc.sync.dma_start(offsets[:], offs)
+
+        z = [keep.tile([P, T + SPARE], F32, name=f"z{r}", tag=f"z{r}") for r in range(PACK)]
+        zeros = keep.tile([P, SPARE], F32)
+        nc.gpsimd.memset(zeros[:], 0.0)
+        for r in range(PACK):
+            nc.scalar.activation(z[r][:, T:], zeros[:], ACT.Copy)
+
+        lam_sb = keep.tile([P, PACK], F32)
+        nc.gpsimd.dma_start(out=lam_sb[:], in_=lam.rearrange("(p r) one -> p (r one)", r=PACK))
+        ident = keep.tile([P, P], F32)
+        make_identity(nc, ident[:])
+        mean_factor = keep.tile([P, PACK], F32)
+        nc.gpsimd.tensor_scalar(mean_factor[:], lam_sb[:], -1.0 / GROUP, 0.0, ALU.mult, ALU.add)
+
+        w_codes = keep.tile([P, PACK, 2 * P], U8, align_bytes=64)
+        nc.vector.tensor_copy(
+            out=w_codes[:].bitcast(U16),
+            in_=w_words_raw[:].bitcast(U16).rearrange("p (q r) -> p r q", r=PACK),
+        )
+        w_plane = keep.tile([P, PACK, P], U8, align_bytes=64)
+        nc.vector.tensor_copy(out=w_plane[:], in_=w_scales_raw[:].rearrange("p (q r) -> p r q", r=PACK))
+
+        banks = [psum.tile([P, T], F32, name=f"zbank{r}") for r in range(1, PACK)]
+        for s in range(pieces):
+            grouped = keep.tile([P, TOKEN_PIECE, PACK], BF16, name=f"x_grouped{s}", align_bytes=64)
+            nc.vector.tensor_copy(out=grouped[:, :VECTOR_TOKENS, :], in_=x_raw[s][:, :, :VECTOR_TOKENS].rearrange("p j t -> p t j"))
+            nc.scalar.activation(grouped[:, VECTOR_TOKENS:, :], x_raw[s][:, :, VECTOR_TOKENS:].rearrange("p j t -> p t j"), ACT.Copy)
+            x_codes = keep.tile([P, TOKEN_PIECE], U32, name=f"x_codes{s}", align_bytes=64)
+            x_plane = keep.tile([P, TOKEN_PIECE], U8, name=f"x_plane{s}", align_bytes=64)
+            nc.vector.quantize_mx(out=x_codes[:].bitcast(FP8X4), scales=x_plane[:], in_=grouped[:].rearrange("p t j -> p (t j)"))
+            cols = slice(s * TOKEN_PIECE, (s + 1) * TOKEN_PIECE)
+            first = psum.tile([P, TOKEN_PIECE], F32, name=f"first{s}", tag=f"sums{s}")
+            for r in range(PACK):
+                nc.tensor.matmul_mx(
+                    out=first[:] if r == 0 else banks[r - 1][:, cols],
+                    lhsT=w_codes[:, r, :].bitcast(FP4X4),
+                    lhsT_scale=w_plane[:, r, :],
+                    rhs=x_codes[:].bitcast(FP8X4),
+                    rhs_scale=x_plane[:],
+                    start=True,
+                    stop=True,
+                )
+            nc.scalar.activation(z[0][:, cols], first[:], ACT.Copy)
+        for r in range(1, PACK):
+            nc.scalar.activation(z[r][:, :T], banks[r - 1][:], ACT.Copy)
+
+        u = [keep.tile([P, J], F32, name=f"u{r}") for r in range(PACK)]
+        mean_term = keep.tile([P, PACK, B], F32)
+        for r in range(PACK):
+            for h in range(HALVES):
+                nc.vector.tensor_copy(u[r][:, h * HALF_J : (h + 1) * HALF_J], z[r][:].indirect(offsets[:, h * HALF_J // 16 : (h + 1) * HALF_J // 16]))
+            slots = u[r][:].rearrange("p (b i) -> p b i", i=GROUP)
+            turned = psum.tile([P, P], F32, name=f"turned{r % 2}")
+            for i in range(GROUP):
+                nc.tensor.matmul(turned[:], slots[:, :, i], ident[:], start=(i == 0), stop=(i == GROUP - 1), is_transpose=True)
+            turned_sb = keep.tile([P, P], F32, name=f"turned_sb{r}")
+            nc.scalar.activation(turned_sb[:], turned[:], ACT.Copy)
+            sums = psum.tile([P, B], F32, name=f"sums{r}", tag=f"sums{r % 2}")
+            nc.tensor.transpose(sums[:], turned_sb[:], ident[:])
+            nc.scalar.activation(mean_term[:, r, :], sums[:], ACT.Copy, scale=mean_factor[:, r : r + 1])
+
+        peaks = keep.tile([P, PACK, B], F32, name="peaks", tag="z3")
+        y = keep.tile([P, PACK, B], F32)
+        y_grouped = keep.tile([P, B, PACK], BF16, align_bytes=64)
+        y_rows = out_0.rearrange("(p r) b -> p r b", r=PACK)
+        for r, bs in ((0, slice(0, B)), (1, slice(0, B)), (2, slice(0, B)), (3, slice(0, HALF_B)), (3, slice(HALF_B, B))):
+            nc.vector.tensor_reduce(peaks[:, r, bs], u[r][:].rearrange("p (b i) -> p b i", i=GROUP)[:, bs, :], mybir.AxisListType.X, ALU.max)
+        nc.gpsimd.tensor_tensor(y[:, 0:2, :], peaks[:, 0:2, :], mean_term[:, 0:2, :], ALU.add)
+        nc.scalar.activation(y_grouped[:, :, 0:2], y[:, 0:2, :].rearrange("p r b -> p b r"), ACT.Copy)
+        nc.sync.dma_start(out=y_rows[:, 0:2, :], in_=y[:, 0:2, :])
+        for h in range(HALVES):
+            bs = slice(h * HALF_B, (h + 1) * HALF_B)
+            nc.vector.tensor_tensor(
+                y_grouped[:, bs, 2:4], peaks[:, 2:4, bs].rearrange("p r b -> p b r"), mean_term[:, 2:4, bs].rearrange("p r b -> p b r"), ALU.add
+            )
+        nc.vector.tensor_tensor(y[:, 2:4, :], peaks[:, 2:4, :], mean_term[:, 2:4, :], ALU.add)
+        nc.sync.dma_start(out=y_rows[:, 2:4, :], in_=y[:, 2:4, :])
+
+        y_codes = keep.tile([P, B], U32, align_bytes=64)
+        y_plane = keep.tile([P, B], U8, align_bytes=64)
+        nc.vector.quantize_mx(out=y_codes[:].bitcast(FP8X4), scales=y_plane[:], in_=y_grouped[:].rearrange("p b r -> p (b r)"))
+        nc.sync.dma_start(out=out_1[0].rearrange("p c r -> p (c r)").bitcast(I32), in_=y_codes[:].bitcast(I32))
+        for q in range(4):
+            queue = nc.scalar if q % 2 == 0 else nc.sync
+            queue.dma_start(out=out_2[0, 4 * q : 4 * q + 4, :].bitcast(I32), in_=y_plane[32 * q : 32 * q + 4, :].bitcast(I32))

@@ -24,8 +24,8 @@ HALVES = 2
 HALF_J = J // HALVES
 HALF_B = B // HALVES
 SPARE = 8
-TOKEN_PIECE = 256
-VECTOR_TOKENS = 160
+EARLY = 384
+VECTOR_TOKENS = 256
 
 
 def tile_list_head_peaks_of_groups_pl_kernel(tc, xt, w_words, w_scales, lam, offs, out_0, out_1, out_2):
@@ -35,25 +35,22 @@ def tile_list_head_peaks_of_groups_pl_kernel(tc, xt, w_words, w_scales, lam, off
         keep = ctx.enter_context(tc.tile_pool(name="keep", bufs=1))
         psum = ctx.enter_context(tc.psum_pool(name="psum", bufs=1))
 
-        pieces = T // TOKEN_PIECE
         x_rows = xt.rearrange("(p j) t -> p j t", j=PACK)
-        x_raw = []
-        for s in range(pieces):
-            raw = keep.tile([P, PACK, TOKEN_PIECE], F32, name=f"x_raw{s}")
-            nc.scalar.dma_start(out=raw[:], in_=x_rows[:, :, s * TOKEN_PIECE : (s + 1) * TOKEN_PIECE])
-            x_raw.append(raw)
-
+        x_early = keep.tile([P, PACK, EARLY], F32)
+        x_late = keep.tile([P, PACK, T - EARLY], F32)
         w_scales_raw = keep.tile([P, N], U8, align_bytes=64)
         nc.gpsimd.memset(w_scales_raw[:].bitcast(I32), 0)
         w_words_raw = keep.tile([P, 2 * N], U8, align_bytes=64)
         nc.sync.dma_start(out=w_words_raw[:].bitcast(I32), in_=w_words[0].bitcast(I32))
+        nc.scalar.dma_start(out=x_early[:], in_=x_rows[:, :, :EARLY])
+        offsets = lists.tile([P, J // 16], U16, name="offsets")
+        nc.sync.dma_start(offsets[:], offs)
         for q in range(4):
             nc.sync.dma_start(
                 out=w_scales_raw[32 * q : 32 * q + 4, :].bitcast(I32),
                 in_=w_scales[0, 4 * q : 4 * q + 4, :].bitcast(I32),
             )
-        offsets = lists.tile([P, J // 16], U16, name="offsets")
-        nc.sync.dma_start(offsets[:], offs)
+        nc.sync.dma_start(out=x_late[:], in_=x_rows[:, :, EARLY:])
 
         z = [keep.tile([P, T + SPARE], F32, name=f"z{r}", tag=f"z{r}") for r in range(PACK)]
         zeros = keep.tile([P, SPARE], F32)
@@ -76,40 +73,57 @@ def tile_list_head_peaks_of_groups_pl_kernel(tc, xt, w_words, w_scales, lam, off
         w_plane = keep.tile([P, PACK, P], U8, align_bytes=64)
         nc.vector.tensor_copy(out=w_plane[:], in_=w_scales_raw[:].rearrange("p (q r) -> p r q", r=PACK))
 
-        banks = [psum.tile([P, T], F32, name=f"zbank{r}") for r in range(1, PACK)]
-        for s in range(pieces):
-            grouped = keep.tile([P, TOKEN_PIECE, PACK], BF16, name=f"x_grouped{s}", align_bytes=64)
-            nc.vector.tensor_copy(out=grouped[:, :VECTOR_TOKENS, :], in_=x_raw[s][:, :, :VECTOR_TOKENS].rearrange("p j t -> p t j"))
-            nc.scalar.activation(grouped[:, VECTOR_TOKENS:, :], x_raw[s][:, :, VECTOR_TOKENS:].rearrange("p j t -> p t j"), ACT.Copy)
-            x_codes = keep.tile([P, TOKEN_PIECE], U32, name=f"x_codes{s}", align_bytes=64)
-            x_plane = keep.tile([P, TOKEN_PIECE], U8, name=f"x_plane{s}", align_bytes=64)
-            nc.vector.quantize_mx(out=x_codes[:].bitcast(FP8X4), scales=x_plane[:], in_=grouped[:].rearrange("p t j -> p (t j)"))
-            cols = slice(s * TOKEN_PIECE, (s + 1) * TOKEN_PIECE)
-            first = psum.tile([P, TOKEN_PIECE], F32, name=f"first{s}", tag=f"sums{s}")
-            for r in range(PACK):
-                nc.tensor.matmul_mx(
-                    out=first[:] if r == 0 else banks[r - 1][:, cols],
-                    lhsT=w_codes[:, r, :].bitcast(FP4X4),
-                    lhsT_scale=w_plane[:, r, :],
-                    rhs=x_codes[:].bitcast(FP8X4),
-                    rhs_scale=x_plane[:],
-                    start=True,
-                    stop=True,
-                )
-            nc.scalar.activation(z[0][:, cols], first[:], ACT.Copy)
+        x_grouped = keep.tile([P, T, PACK], BF16, align_bytes=64)
+        x_codes = keep.tile([P, T], U32, align_bytes=64)
+        x_plane = keep.tile([P, T], U8, align_bytes=64)
+        nc.vector.tensor_copy(out=x_grouped[:, :VECTOR_TOKENS, :], in_=x_early[:, :, :VECTOR_TOKENS].rearrange("p j t -> p t j"))
+        nc.scalar.activation(x_grouped[:, VECTOR_TOKENS:EARLY, :], x_early[:, :, VECTOR_TOKENS:].rearrange("p j t -> p t j"), ACT.Copy)
+        nc.scalar.activation(x_grouped[:, EARLY:, :], x_late[:].rearrange("p j t -> p t j"), ACT.Copy)
+        spans = (slice(0, VECTOR_TOKENS), slice(VECTOR_TOKENS, EARLY), slice(EARLY, T))
+        for cols in spans:
+            nc.vector.quantize_mx(
+                out=x_codes[:, cols].bitcast(FP8X4), scales=x_plane[:, cols], in_=x_grouped[:, cols, :].rearrange("p t j -> p (t j)")
+            )
+
+        def product(out, r, cols):
+            nc.tensor.matmul_mx(
+                out=out,
+                lhsT=w_codes[:, r, :].bitcast(FP4X4),
+                lhsT_scale=w_plane[:, r, :],
+                rhs=x_codes[:, cols].bitcast(FP8X4),
+                rhs_scale=x_plane[:, cols],
+                start=True,
+                stop=True,
+            )
+
+        first_early = psum.tile([P, EARLY], F32, name="first_early", tag="sums0")
+        first_late = psum.tile([P, T - EARLY], F32, name="first_late", tag="sums1")
+        product(first_early[:, spans[0]], 0, spans[0])
+        product(first_early[:, spans[1]], 0, spans[1])
+        nc.scalar.activation(z[0][:, :EARLY], first_early[:], ACT.Copy)
+        product(first_late[:], 0, spans[2])
+        nc.scalar.activation(z[0][:, EARLY:T], first_late[:], ACT.Copy)
         for r in range(1, PACK):
-            nc.scalar.activation(z[r][:, :T], banks[r - 1][:], ACT.Copy)
+            bank = psum.tile([P, T], F32, name=f"zbank{r}")
+            product(bank[:], r, slice(0, T))
+            nc.scalar.activation(z[r][:, :T], bank[:], ACT.Copy)
 
         u = [keep.tile([P, J], F32, name=f"u{r}") for r in range(PACK)]
         mean_term = keep.tile([P, PACK, B], F32)
         for r in range(PACK):
+            slots = keep.tile([P, GROUP, B], F32, name=f"slots{r}")
             for h in range(HALVES):
-                nc.vector.tensor_copy(u[r][:, h * HALF_J : (h + 1) * HALF_J], z[r][:].indirect(offsets[:, h * HALF_J // 16 : (h + 1) * HALF_J // 16]))
-            slots = u[r][:].rearrange("p (b i) -> p b i", i=GROUP)
+                picked = u[r][:, h * HALF_J : (h + 1) * HALF_J]
+                nc.vector.tensor_copy(picked, z[r][:].indirect(offsets[:, h * HALF_J // 16 : (h + 1) * HALF_J // 16]))
+                nc.scalar.activation(
+                    slots[:, :, h * HALF_B : (h + 1) * HALF_B].rearrange("p (k i) b -> p k b i", i=4),
+                    picked.rearrange("p (b k i) -> p k b i", k=2, i=4),
+                    ACT.Copy,
+                )
             turned = psum.tile([P, P], F32, name=f"turned{r % 2}")
             for i in range(GROUP):
-                nc.tensor.matmul(turned[:], slots[:, :, i], ident[:], start=(i == 0), stop=(i == GROUP - 1), is_transpose=True)
-            turned_sb = keep.tile([P, P], F32, name=f"turned_sb{r}")
+                nc.tensor.matmul(turned[:], slots[:, i, :], ident[:], start=(i == 0), stop=(i == GROUP - 1), is_transpose=True)
+            turned_sb = keep.tile([P, P], F32, name=f"turned_sb{r}", tag=f"turned_sb{r}", align_bytes=64)
             nc.scalar.activation(turned_sb[:], turned[:], ACT.Copy)
             sums = psum.tile([P, B], F32, name=f"sums{r}", tag=f"sums{r % 2}")
             nc.tensor.transpose(sums[:], turned_sb[:], ident[:])
@@ -117,7 +131,7 @@ def tile_list_head_peaks_of_groups_pl_kernel(tc, xt, w_words, w_scales, lam, off
 
         peaks = keep.tile([P, PACK, B], F32, name="peaks", tag="z3")
         y = keep.tile([P, PACK, B], F32)
-        y_grouped = keep.tile([P, B, PACK], BF16, align_bytes=64)
+        y_grouped = keep.tile([P, B, PACK], BF16, name="y_grouped", tag="turned_sb3", align_bytes=64)
         y_rows = out_0.rearrange("(p r) b -> p r b", r=PACK)
         for r, bs in ((0, slice(0, B)), (1, slice(0, B)), (2, slice(0, B)), (3, slice(0, HALF_B)), (3, slice(HALF_B, B))):
             nc.vector.tensor_reduce(peaks[:, r, bs], u[r][:].rearrange("p (b i) -> p b i", i=GROUP)[:, bs, :], mybir.AxisListType.X, ALU.max)

@@ -110,6 +110,7 @@ def tile_list_head_peaks_of_groups_pl_kernel(tc, xt, w_words, w_scales, lam, off
 
         u = [keep.tile([P, J], F32, name=f"u{r}") for r in range(PACK)]
         mean_term = keep.tile([P, PACK, B], F32)
+        fours = keep.tile([P, 2, B, 4], F32)
         for r in range(PACK):
             slots = keep.tile([P, GROUP, B], F32, name=f"slots{r}")
             for h in range(HALVES):
@@ -120,6 +121,12 @@ def tile_list_head_peaks_of_groups_pl_kernel(tc, xt, w_words, w_scales, lam, off
                     picked.rearrange("p (b k i) -> p k b i", k=2, i=4),
                     ACT.Copy,
                 )
+            if r < 2:
+                pairs = u[r][:].rearrange("p (b k i) -> p k b i", k=2, i=4)
+                excess = keep.tile([P, B, 4], F32, name=f"excess{r}", tag=f"excess{r}")
+                nc.gpsimd.tensor_tensor(excess[:], pairs[:, 0], pairs[:, 1], ALU.subtract)
+                nc.scalar.activation(excess[:], excess[:], ACT.Relu)
+                nc.gpsimd.tensor_tensor(fours[:, r], excess[:], pairs[:, 1], ALU.add)
             turned = psum.tile([P, P], F32, name=f"turned{r % 2}")
             for i in range(GROUP):
                 nc.tensor.matmul(turned[:], slots[:, i, :], ident[:], start=(i == 0), stop=(i == GROUP - 1), is_transpose=True)
@@ -129,21 +136,24 @@ def tile_list_head_peaks_of_groups_pl_kernel(tc, xt, w_words, w_scales, lam, off
             nc.tensor.transpose(sums[:], turned_sb[:], ident[:])
             nc.scalar.activation(mean_term[:, r, :], sums[:], ACT.Copy, scale=mean_factor[:, r : r + 1])
 
-        peaks = keep.tile([P, PACK, B], F32, name="peaks", tag="z3")
+        peaks = keep.tile([P, 2, B], F32, name="peaks", tag="z3")
+        late_peaks = keep.tile([P, 2, B], F32, name="late_peaks", tag="excess1")
         y = keep.tile([P, PACK, B], F32)
         y_grouped = keep.tile([P, B, PACK], BF16, name="y_grouped", tag="turned_sb3", align_bytes=64)
         y_rows = out_0.rearrange("(p r) b -> p r b", r=PACK)
-        for r, bs in ((0, slice(0, B)), (1, slice(0, B)), (2, slice(0, B)), (3, slice(0, HALF_B)), (3, slice(HALF_B, B))):
-            nc.vector.tensor_reduce(peaks[:, r, bs], u[r][:].rearrange("p (b i) -> p b i", i=GROUP)[:, bs, :], mybir.AxisListType.X, ALU.max)
-        nc.gpsimd.tensor_tensor(y[:, 0:2, :], peaks[:, 0:2, :], mean_term[:, 0:2, :], ALU.add)
+        nc.vector.tensor_reduce(peaks[:], fours[:], mybir.AxisListType.X, ALU.max)
+        nc.vector.tensor_reduce(late_peaks[:, 0, :], u[2][:].rearrange("p (b i) -> p b i", i=GROUP), mybir.AxisListType.X, ALU.max)
+        for bs in (slice(0, HALF_B), slice(HALF_B, B)):
+            nc.vector.tensor_reduce(late_peaks[:, 1, bs], u[3][:].rearrange("p (b i) -> p b i", i=GROUP)[:, bs, :], mybir.AxisListType.X, ALU.max)
+        nc.gpsimd.tensor_tensor(y[:, 0:2, :], peaks[:], mean_term[:, 0:2, :], ALU.add)
         nc.scalar.activation(y_grouped[:, :, 0:2], y[:, 0:2, :].rearrange("p r b -> p b r"), ACT.Copy)
         nc.sync.dma_start(out=y_rows[:, 0:2, :], in_=y[:, 0:2, :])
         for h in range(HALVES):
             bs = slice(h * HALF_B, (h + 1) * HALF_B)
             nc.vector.tensor_tensor(
-                y_grouped[:, bs, 2:4], peaks[:, 2:4, bs].rearrange("p r b -> p b r"), mean_term[:, 2:4, bs].rearrange("p r b -> p b r"), ALU.add
+                y_grouped[:, bs, 2:4], late_peaks[:, :, bs].rearrange("p r b -> p b r"), mean_term[:, 2:4, bs].rearrange("p r b -> p b r"), ALU.add
             )
-        nc.vector.tensor_tensor(y[:, 2:4, :], peaks[:, 2:4, :], mean_term[:, 2:4, :], ALU.add)
+        nc.vector.tensor_tensor(y[:, 2:4, :], late_peaks[:], mean_term[:, 2:4, :], ALU.add)
         nc.sync.dma_start(out=y_rows[:, 2:4, :], in_=y[:, 2:4, :])
 
         y_codes = keep.tile([P, B], U32, align_bytes=64)

@@ -109,35 +109,49 @@ def tile_list_head_peaks_of_groups_pl_kernel(tc, xt, w_words, w_scales, lam, off
             nc.scalar.activation(z[r][:, :T], bank[:], ACT.Copy)
 
         u = [keep.tile([P, J], F32, name=f"u{r}") for r in range(PACK)]
-        mean_term = keep.tile([P, PACK, B], F32)
-        fours = keep.tile([P, 2, B, 4], F32)
+        mean_term = keep.tile([P, 2, B], F32)
+        late_mean_term = psum.tile([P, 2, B], F32)
+        gains = []
         for r in range(PACK):
-            slots = keep.tile([P, GROUP, B], F32, name=f"slots{r}")
-            for h in range(HALVES):
-                picked = u[r][:, h * HALF_J : (h + 1) * HALF_J]
-                nc.vector.tensor_copy(picked, z[r][:].indirect(offsets[:, h * HALF_J // 16 : (h + 1) * HALF_J // 16]))
-                nc.scalar.activation(
-                    slots[:, :, h * HALF_B : (h + 1) * HALF_B].rearrange("p (k i) b -> p k b i", i=4),
-                    picked.rearrange("p (b k i) -> p k b i", k=2, i=4),
-                    ACT.Copy,
-                )
+            cuts = (0, J // 2, 3 * J // 4, J) if r == PACK - 1 else (0, J // 2, J)
+            if r == 0:
+                slots = u[r][:].rearrange("p (b i) -> p i b", i=GROUP)
+            else:
+                slots = keep.tile([P, GROUP, B], F32, name=f"slots{r}", tag="excess1" if r == 3 else f"slots{r}", align_bytes=64)[:]
+            for lo, hi in zip(cuts[:-1], cuts[1:]):
+                nc.vector.tensor_copy(u[r][:, lo:hi], z[r][:].indirect(offsets[:, lo // 16 : hi // 16]))
+                if r > 0:
+                    nc.scalar.activation(
+                        slots[:, :, lo // GROUP : hi // GROUP].rearrange("p (k i) b -> p k b i", i=4),
+                        u[r][:, lo:hi].rearrange("p (b k i) -> p k b i", k=2, i=4),
+                        ACT.Copy,
+                        scale=mean_factor[:, r : r + 1],
+                    )
             if r < 2:
                 pairs = u[r][:].rearrange("p (b k i) -> p k b i", k=2, i=4)
-                excess = keep.tile([P, B, 4], F32, name=f"excess{r}", tag=f"excess{r}")
+                excess = keep.tile([P, B, 4], F32, name=f"excess{r}", tag=f"excess{r}", align_bytes=64)
+                gain = keep.tile([P, B, 4], F32, name=f"gain{r}", tag=f"gain{r}")
                 nc.gpsimd.tensor_tensor(excess[:], pairs[:, 0], pairs[:, 1], ALU.subtract)
-                nc.scalar.activation(excess[:], excess[:], ACT.Relu)
-                nc.gpsimd.tensor_tensor(fours[:, r], excess[:], pairs[:, 1], ALU.add)
+                nc.scalar.activation(gain[:], excess[:], ACT.Relu)
+                gains.append((gain, pairs))
+            if r == 1:
+                fours = keep.tile([P, 2, B, 4], F32, name="fours", tag="z1")
+                for e in range(2):
+                    nc.gpsimd.tensor_tensor(fours[:, e], gains[e][0][:], gains[e][1][:, 1], ALU.add)
             turned = psum.tile([P, P], F32, name=f"turned{r % 2}")
             for i in range(GROUP):
                 nc.tensor.matmul(turned[:], slots[:, i, :], ident[:], start=(i == 0), stop=(i == GROUP - 1), is_transpose=True)
             turned_sb = keep.tile([P, P], F32, name=f"turned_sb{r}", tag=f"turned_sb{r}", align_bytes=64)
             nc.scalar.activation(turned_sb[:], turned[:], ACT.Copy)
-            sums = psum.tile([P, B], F32, name=f"sums{r}", tag=f"sums{r % 2}")
-            nc.tensor.transpose(sums[:], turned_sb[:], ident[:])
-            nc.scalar.activation(mean_term[:, r, :], sums[:], ACT.Copy, scale=mean_factor[:, r : r + 1])
+            if r < 2:
+                sums = psum.tile([P, B], F32, name=f"sums{r}", tag=f"sums{r}")
+                nc.tensor.transpose(sums[:], turned_sb[:], ident[:])
+                nc.scalar.activation(mean_term[:, r, :], sums[:], ACT.Copy, scale=mean_factor[:, 0:1] if r == 0 else 1.0)
+            else:
+                nc.tensor.transpose(late_mean_term[:, r - 2, :], turned_sb[:], ident[:])
 
         peaks = keep.tile([P, 2, B], F32, name="peaks", tag="z3")
-        late_peaks = keep.tile([P, 2, B], F32, name="late_peaks", tag="excess1")
+        late_peaks = keep.tile([P, 2, B], F32, name="late_peaks", tag="gain1")
         y = keep.tile([P, PACK, B], F32)
         y_grouped = keep.tile([P, B, PACK], BF16, name="y_grouped", tag="turned_sb3", align_bytes=64)
         y_rows = out_0.rearrange("(p r) b -> p r b", r=PACK)
@@ -145,15 +159,15 @@ def tile_list_head_peaks_of_groups_pl_kernel(tc, xt, w_words, w_scales, lam, off
         nc.vector.tensor_reduce(late_peaks[:, 0, :], u[2][:].rearrange("p (b i) -> p b i", i=GROUP), mybir.AxisListType.X, ALU.max)
         for bs in (slice(0, HALF_B), slice(HALF_B, B)):
             nc.vector.tensor_reduce(late_peaks[:, 1, bs], u[3][:].rearrange("p (b i) -> p b i", i=GROUP)[:, bs, :], mybir.AxisListType.X, ALU.max)
-        nc.gpsimd.tensor_tensor(y[:, 0:2, :], peaks[:], mean_term[:, 0:2, :], ALU.add)
+        nc.gpsimd.tensor_tensor(y[:, 0:2, :], peaks[:], mean_term[:], ALU.add)
         nc.scalar.activation(y_grouped[:, :, 0:2], y[:, 0:2, :].rearrange("p r b -> p b r"), ACT.Copy)
         nc.sync.dma_start(out=y_rows[:, 0:2, :], in_=y[:, 0:2, :])
         for h in range(HALVES):
             bs = slice(h * HALF_B, (h + 1) * HALF_B)
             nc.vector.tensor_tensor(
-                y_grouped[:, bs, 2:4], late_peaks[:, :, bs].rearrange("p r b -> p b r"), mean_term[:, 2:4, bs].rearrange("p r b -> p b r"), ALU.add
+                y_grouped[:, bs, 2:4], late_peaks[:, :, bs].rearrange("p r b -> p b r"), late_mean_term[:, :, bs].rearrange("p r b -> p b r"), ALU.add
             )
-        nc.vector.tensor_tensor(y[:, 2:4, :], late_peaks[:], mean_term[:, 2:4, :], ALU.add)
+        nc.vector.tensor_tensor(y[:, 2:4, :], late_peaks[:], late_mean_term[:], ALU.add)
         nc.sync.dma_start(out=y_rows[:, 2:4, :], in_=y[:, 2:4, :])
 
         y_codes = keep.tile([P, B], U32, align_bytes=64)

from contextlib import ExitStack

import concourse.mybir as mybir
from concourse.masks import make_identity

K, T, J, N, B = 512, 512, 1024, 512, 128
FLOPS = 2 * K * N * T

F32 = mybir.dt.float32
BF16 = mybir.dt.bfloat16
I32 = mybir.dt.int32
U32 = mybir.dt.uint32
U16 = mybir.dt.uint16
U8 = mybir.dt.uint8
FP8X4 = mybir.dt.float8_e4m3fn_x4
FP4X4 = mybir.dt.float4_e2m1fn_x4
ALU = mybir.AluOpType
ACT = mybir.ActivationFunctionType

P = 128
PACK = 4
GROUP = J // B
HALVES = 2
HALF_J = J // HALVES
HALF_B = B // HALVES
SPARE = 8
EARLY = 384
VECTOR_TOKENS = 256


def tile_list_head_peaks_of_groups_pl_kernel(tc, xt, w_words, w_scales, lam, offs, out_0, out_1, out_2):
    nc = tc.nc
    with ExitStack() as ctx:
        lists = ctx.enter_context(tc.tile_pool(name="lists", bufs=1))
        keep = ctx.enter_context(tc.tile_pool(name="keep", bufs=1))
        psum = ctx.enter_context(tc.psum_pool(name="psum", bufs=1))

        x_rows = xt.rearrange("(p j) t -> p j t", j=PACK)
        x_early = keep.tile([P, PACK, EARLY], F32)
        x_late = keep.tile([P, PACK, T - EARLY], F32)
        w_scales_raw = keep.tile([P, N], U8, align_bytes=64)
        nc.gpsimd.memset(w_scales_raw[:].bitcast(I32), 0)
        w_words_raw = keep.tile([P, 2 * N], U8, align_bytes=64)
        nc.sync.dma_start(out=w_words_raw[:].bitcast(I32), in_=w_words[0].bitcast(I32))
        nc.scalar.dma_start(out=x_early[:], in_=x_rows[:, :, :EARLY])
        offsets = lists.tile([P, J // 16], U16, name="offsets")
        nc.sync.dma_start(offsets[:], offs)
        for q in range(4):
            nc.sync.dma_start(
                out=w_scales_raw[32 * q : 32 * q + 4, :].bitcast(I32),
                in_=w_scales[0, 4 * q : 4 * q + 4, :].bitcast(I32),
            )
        nc.sync.dma_start(out=x_late[:], in_=x_rows[:, :, EARLY:])

        z = [keep.tile([P, T + SPARE], F32, name=f"z{r}", tag=f"z{r}") for r in range(PACK)]
        zeros = keep.tile([P, SPARE], F32)
        nc.gpsimd.memset(zeros[:], 0.0)
        for r in range(PACK):
            nc.scalar.activation(z[r][:, T:], zeros[:], ACT.Copy)

        lam_sb = keep.tile([P, PACK], F32)
        nc.gpsimd.dma_start(out=lam_sb[:], in_=lam.rearrange("(p r) one -> p (r one)", r=PACK))
        ident = keep.tile([P, P], F32)
        make_identity(nc, ident[:])
        mean_factor = keep.tile([P, PACK], F32)
        nc.gpsimd.tensor_scalar(mean_factor[:], lam_sb[:], -1.0 / GROUP, 0.0, ALU.mult, ALU.add)

        w_codes = keep.tile([P, PACK, 2 * P], U8, align_bytes=64)
        nc.vector.tensor_copy(
            out=w_codes[:].bitcast(U16),
            in_=w_words_raw[:].bitcast(U16).rearrange("p (q r) -> p r q", r=PACK),
        )
        w_plane = keep.tile([P, PACK, P], U8, align_bytes=64)
        nc.vector.tensor_copy(out=w_plane[:], in_=w_scales_raw[:].rearrange("p (q r) -> p r q", r=PACK))

        x_grouped = keep.tile([P, T, PACK], BF16, align_bytes=64)
        x_codes = keep.tile([P, T], U32, align_bytes=64)
        x_plane = keep.tile([P, T], U8, align_bytes=64)
        nc.vector.tensor_copy(out=x_grouped[:, :VECTOR_TOKENS, :], in_=x_early[:, :, :VECTOR_TOKENS].rearrange("p j t -> p t j"))
        nc.scalar.activation(x_grouped[:, VECTOR_TOKENS:EARLY, :], x_early[:, :, VECTOR_TOKENS:].rearrange("p j t -> p t j"), ACT.Copy)
        nc.scalar.activation(x_grouped[:, EARLY:, :], x_late[:].rearrange("p j t -> p t j"), ACT.Copy)
        spans = (slice(0, VECTOR_TOKENS), slice(VECTOR_TOKENS, EARLY), slice(EARLY, T))
        for cols in spans:
            nc.vector.quantize_mx(
                out=x_codes[:, cols].bitcast(FP8X4), scales=x_plane[:, cols], in_=x_grouped[:, cols, :].rearrange("p t j -> p (t j)")
            )

        def product(out, r, cols):
            nc.tensor.matmul_mx(
                out=out,
                lhsT=w_codes[:, r, :].bitcast(FP4X4),
                lhsT_scale=w_plane[:, r, :],
                rhs=x_codes[:, cols].bitcast(FP8X4),
                rhs_scale=x_plane[:, cols],
                start=True,
                stop=True,
            )

        first_early = psum.tile([P, EARLY], F32, name="first_early", tag="sums0")
        first_late = psum.tile([P, T - EARLY], F32, name="first_late", tag="sums1")
        product(first_early[:, spans[0]], 0, spans[0])
        product(first_early[:, spans[1]], 0, spans[1])
        nc.scalar.activation(z[0][:, :EARLY], first_early[:], ACT.Copy)
        product(first_late[:], 0, spans[2])
        nc.scalar.activation(z[0][:, EARLY:T], first_late[:], ACT.Copy)
        for r in range(1, PACK):
            bank = psum.tile([P, T], F32, name=f"zbank{r}")
            product(bank[:], r, slice(0, T))
            nc.scalar.activation(z[r][:, :T], bank[:], ACT.Copy)

        u = [keep.tile([P, J], F32, name=f"u{r}") for r in range(PACK)]
        mean_term = keep.tile([P, 2, B], F32)
        late_mean_term = psum.tile([P, 2, B], F32)
        gains = []
        for r in range(PACK):
            cuts = (0, J // 2, 3 * J // 4, J) if r == PACK - 1 else (0, J // 2, J)
            if r == 0:
                slots = u[r][:].rearrange("p (b i) -> p i b", i=GROUP)
            else:
                slots = keep.tile([P, GROUP, B], F32, name=f"slots{r}", tag="excess1" if r == 3 else f"slots{r}", align_bytes=64)[:]
            for lo, hi in zip(cuts[:-1], cuts[1:]):
                nc.vector.tensor_copy(u[r][:, lo:hi], z[r][:].indirect(offsets[:, lo // 16 : hi // 16]))
                if r > 0:
                    nc.scalar.activation(
                        slots[:, :, lo // GROUP : hi // GROUP].rearrange("p (k i) b -> p k b i", i=4),
                        u[r][:, lo:hi].rearrange("p (b k i) -> p k b i", k=2, i=4),
                        ACT.Copy,
                        scale=mean_factor[:, r : r + 1],
                    )
            if r < 2:
                pairs = u[r][:].rearrange("p (b k i) -> p k b i", k=2, i=4)
                excess = keep.tile([P, B, 4], F32, name=f"excess{r}", tag=f"excess{r}", align_bytes=64)
                gain = keep.tile([P, B, 4], F32, name=f"gain{r}", tag=f"gain{r}")
                nc.gpsimd.tensor_tensor(excess[:], pairs[:, 0], pairs[:, 1], ALU.subtract)
                nc.scalar.activation(gain[:], excess[:], ACT.Relu)
                gains.append((gain, pairs))
            if r == 1:
                fours = keep.tile([P, 2, B, 4], F32, name="fours", tag="z1")
                for e in range(2):
                    nc.gpsimd.tensor_tensor(fours[:, e], gains[e][0][:], gains[e][1][:, 1], ALU.add)
            turned = psum.tile([P, P], F32, name=f"turned{r % 2}")
            for i in range(GROUP):
                nc.tensor.matmul(turned[:], slots[:, i, :], ident[:], start=(i == 0), stop=(i == GROUP - 1), is_transpose=True)
            turned_sb = keep.tile([P, P], F32, name=f"turned_sb{r}", tag=f"turned_sb{r}", align_bytes=64)
            nc.scalar.activation(turned_sb[:], turned[:], ACT.Copy)
            if r < 2:
                sums = psum.tile([P, B], F32, name=f"sums{r}", tag=f"sums{r}")
                nc.tensor.transpose(sums[:], turned_sb[:], ident[:])
                nc.scalar.activation(mean_term[:, r, :], sums[:], ACT.Copy, scale=mean_factor[:, 0:1] if r == 0 else 1.0)
            else:
                nc.tensor.transpose(late_mean_term[:, r - 2, :], turned_sb[:], ident[:])

        peaks = keep.tile([P, 2, B], F32, name="peaks", tag="z3")
        late_peaks = keep.tile([P, 2, B], F32, name="late_peaks", tag="gain1")
        y = keep.tile([P, PACK, B], F32)
        y_grouped = keep.tile([P, B, PACK], BF16, name="y_grouped", tag="turned_sb3", align_bytes=64)
        y_rows = out_0.rearrange("(p r) b -> p r b", r=PACK)
        nc.vector.tensor_reduce(peaks[:], fours[:], mybir.AxisListType.X, ALU.max)
        nc.vector.tensor_reduce(late_peaks[:, 0, :], u[2][:].rearrange("p (b i) -> p b i", i=GROUP), mybir.AxisListType.X, ALU.max)
        for bs in (slice(0, HALF_B), slice(HALF_B, B)):
            nc.vector.tensor_reduce(late_peaks[:, 1, bs], u[3][:].rearrange("p (b i) -> p b i", i=GROUP)[:, bs, :], mybir.AxisListType.X, ALU.max)
        nc.gpsimd.tensor_tensor(y[:, 0:2, :], peaks[:], mean_term[:], ALU.add)
        nc.scalar.activation(y_grouped[:, :, 0:2], y[:, 0:2, :].rearrange("p r b -> p b r"), ACT.Copy)
        nc.sync.dma_start(out=y_rows[:, 0:2, :], in_=y[:, 0:2, :])
        for h in range(HALVES):
            bs = slice(h * HALF_B, (h + 1) * HALF_B)
            nc.vector.tensor_tensor(
                y_grouped[:, bs, 2:4], late_peaks[:, :, bs].rearrange("p r b -> p b r"), late_mean_term[:, :, bs].rearrange("p r b -> p b r"), ALU.add
            )
        nc.vector.tensor_tensor(y[:, 2:4, :], late_peaks[:], late_mean_term[:], ALU.add)
        nc.sync.dma_start(out=y_rows[:, 2:4, :], in_=y[:, 2:4, :])

        y_codes = keep.tile([P, B], U32, align_bytes=64)
        y_plane = keep.tile([P, B], U8, align_bytes=64)
        nc.vector.quantize_mx(out=y_codes[:].bitcast(FP8X4), scales=y_plane[:], in_=y_grouped[:].rearrange("p b r -> p (b r)"))
        nc.sync.dma_start(out=out_1[0].rearrange("p c r -> p (c r)").bitcast(I32), in_=y_codes[:].bitcast(I32))
        for q in range(4):
            queue = nc.scalar if q % 2 == 0 else nc.sync
            queue.dma_start(out=out_2[0, 4 * q : 4 * q + 4, :].bitcast(I32), in_=y_plane[32 * q : 32 * q + 4, :].bitcast(I32))
